import numpy as np
import ml_dtypes


def mxq(x, axis, fmt="e4m3"):
    dtype, down = {"e4m3": (ml_dtypes.float8_e4m3fn, 7), "e5m2": (ml_dtypes.float8_e5m2, 14)}[fmt]
    v = np.moveaxis(np.asarray(x, np.float32).astype(ml_dtypes.bfloat16).astype(np.float64), axis, -1)
    blocks = v.reshape(v.shape[:-1] + (-1, 32))
    amax = np.abs(blocks).max(-1, keepdims=True)
    byte = np.maximum(np.where(amax > 0, np.frexp(amax)[1] - 1 + 127, 0) - down, 1)
    scale = np.exp2(byte - 127.0)
    codes = (blocks / scale).astype(np.float32).astype(dtype).astype(np.float64)
    return np.moveaxis((codes * scale).reshape(v.shape), -1, axis)


WIDE = False


def mx_kscale(k):
    if not WIDE:
        return np.ones(k)
    levels = np.array([10, -10, 5, -5, 0])
    if k % 512:
        return np.exp2(np.random.permutation(np.resize(levels, k // 32))).repeat(32)
    a = np.empty((k // 512, 16))
    for p in range(k // 512):
        a[p, :8] = np.random.permutation(np.resize(levels, 8))
        for g in range(8):
            far = levels[np.abs(levels - a[p, g]) >= 10]
            a[p, g + 8] = far[np.random.randint(len(far))]
    return np.exp2(a.ravel()).repeat(32)


def f64(x):
    return np.asarray(x).astype(np.float64)


def striped(idx):
    return np.tile(np.asarray(idx).reshape(-1, 16).T, (8, 1)).astype(np.uint16)


def unstriped(offs):
    return offs[:16].T.reshape(-1).astype(np.int64)


E2M1 = np.array([0.0, 0.5, 1.0, 1.5, 2.0, 3.0, 4.0, 6.0, -0.0, -0.5, -1.0, -1.5, -2.0, -3.0, -4.0, -6.0])


def pack_weight(w, fmt):
    k, n = w.shape
    w = f64(np.asarray(w, np.float32).astype(ml_dtypes.bfloat16)).reshape(k // 32, 32, n)
    amax = np.abs(w).max(1)
    if fmt == "e4m3":
        byte = np.frexp(amax)[1] - 1 + 127 - 7
    else:
        mant, ex = np.frexp(amax / 6.0)
        byte = np.where(mant > 0.5, ex, ex - 1) + 127
    byte = np.clip(np.where(amax > 0, byte, 1), 1, 254)
    scaled = (w * np.exp2(127.0 - byte)[:, None, :]).reshape(k, n).astype(np.float32)
    by_word = np.ascontiguousarray(scaled.reshape(k // 512, 128, 4, n).transpose(0, 1, 3, 2))
    if fmt == "e4m3":
        words = by_word.astype(ml_dtypes.float8_e4m3fn).view(np.uint8)
    else:
        c = by_word.astype(ml_dtypes.float4_e2m1fn).view(np.uint8) & 0xF
        words = (c[..., 0::2] | (c[..., 1::2] << 4)).reshape(k // 512, 128, 2 * n)
    return np.ascontiguousarray(words), np.ascontiguousarray(byte.astype(np.uint8).reshape(k // 512, 16, n))


def unpack_weight(words, scales, fmt):
    g, _, n = scales.shape
    words = np.ascontiguousarray(words).reshape(g, 128, n, -1)
    if fmt == "e4m3":
        vals = words.view(ml_dtypes.float8_e4m3fn).astype(np.float64)
    else:
        nib = np.empty((g, 128, n, 4), np.uint8)
        nib[..., 0::2] = words & 0xF
        nib[..., 1::2] = words >> 4
        vals = E2M1[nib]
    vals = vals * np.repeat(np.exp2(scales.astype(np.float64) - 127.0), 8, axis=1)[..., None]
    return vals.transpose(0, 1, 3, 2).reshape(g * 512, n)


def bf(x):
    return np.asarray(x, np.float32).astype(ml_dtypes.bfloat16)


def planes(Y):
    r, m = Y.shape
    b = f64(bf(Y)).reshape(r // 32, 32, m)
    amax = np.abs(b).max(1)
    byte = np.clip(np.where(amax > 0, np.frexp(amax)[1] - 1 + 127 - 7, 1), 1, 254)
    codes = (b * np.exp2(127.0 - byte)[:, None, :]).reshape(r, m).astype(np.float32).astype(ml_dtypes.float8_e4m3fn).view(np.uint8)
    words = codes.reshape(r // 512, 128, 4, m).transpose(0, 1, 3, 2)
    return np.ascontiguousarray(words), np.ascontiguousarray(byte.astype(np.uint8).reshape(r // 512, 16, m))


K, L, J, I, T, N = 2048, 2048, 512, 512, 512, 512


def setup_inputs():
    n = np.random.standard_normal
    idx = np.random.permutation(K)[:J]
    idx2 = np.random.permutation(L)[:I]
    fk = mx_kscale(K)
    fj = mx_kscale(J)
    fi = mx_kscale(I)
    tj = np.ones(K)
    tj[idx] = fj
    ti = np.ones(L)
    ti[idx2] = fi
    xbp = pack_weight(n((K, T)) / fk[:, None], "e2m1")
    wbp = pack_weight(n((K, N)) * 1 / np.sqrt(K) * fk[:, None], "e2m1")
    vop = pack_weight(n((I, N)) * 1 / np.sqrt(I) * fi[:, None], "e4m3")
    return {
        "xb_words": xbp[0],
        "xb_scales": xbp[1],
        "wb_words": wbp[0],
        "wb_scales": wbp[1],
        "xt": (n((T, K)) / tj).astype(np.float32),
        "wo": (n((J, N)) * 1 / np.sqrt(J) * fj[:, None]).astype(np.float32),
        "zt": (n((T, L)) / ti).astype(np.float32),
        "vo_words": vop[0],
        "vo_scales": vop[1],
        "b": (np.random.uniform(-0.5, 0.5, (N, 1))).astype(np.float32),
        "offs": striped(idx),
        "offs2": striped(idx2),
    }


def reference(xb_words, xb_scales, wb_words, wb_scales, xt, wo, zt, vo_words, vo_scales, b, offs, offs2):
    idx = unstriped(offs)
    idx2 = unstriped(offs2)
    xbu = unpack_weight(xb_words, xb_scales, "e2m1")
    wbu = unpack_weight(wb_words, wb_scales, "e2m1")
    vou = unpack_weight(vo_words, vo_scales, "e4m3")
    xo = f64(xt)[:, idx].T
    zo = f64(zt)[:, idx2].T
    woq = mxq(f64(wo), 0, "e4m3")
    xoq = mxq(xo, 0, "e4m3")
    zoq = mxq(zo, 0, "e4m3")
    z = wbu.T @ xbu + woq.T @ xoq + vou.T @ zoq
    y = z + f64(b)
    words, scales = planes(y)
    return y, words, scales

@@ -1,0 +1,217 @@
+from contextlib import ExitStack
+
+import concourse.mybir as mybir
+from concourse.masks import make_identity
+
+K, J, T, N = 2048, 512, 512, 512
+FLOPS = 2 * (K + J + J) * T * N
+
+F32 = mybir.dt.float32
+BF16 = mybir.dt.bfloat16
+I32 = mybir.dt.int32
+U32 = mybir.dt.uint32
+U16 = mybir.dt.uint16
+U8 = mybir.dt.uint8
+FP8X4 = mybir.dt.float8_e4m3fn_x4
+FP4X4 = mybir.dt.float4_e2m1fn_x4
+ACT = mybir.ActivationFunctionType
+ADD = mybir.AluOpType.add
+
+P = 128
+PACK = 4
+PASSES = K // (P * PACK)
+TILES = T // P
+LAST = TILES - 1
+SLOT = 4 * K
+
+
+def load_scale_rows(nc, plane, scales):
+    passes = scales.shape[0]
+    by_row = scales.rearrange("z (q r) c -> r q z c", r=PACK)
+    for r in range(PACK):
+        nc.sync.dma_start(
+            out=plane[r:P:32, :].bitcast(I32).rearrange("q (z c) -> q z c", z=passes),
+            in_=by_row[r].bitcast(I32),
+        )
+
+
+def deal(copy, dealt, raw):
+    copy(
+        out=dealt.rearrange("p (z i m) -> p z i m", i=PACK, m=P),
+        in_=raw.rearrange("p (z m i) -> p z i m", i=PACK, m=P),
+    )
+
+
+def tile_list_outlier_streams_pl_kernel(
+    tc, xb_words, xb_scales, wb_words, wb_scales, xt, wo, zt, vo_words, vo_scales, b, offs, offs2, out_0, out_1, out_2
+):
+    nc = tc.nc
+    with ExitStack() as ctx:
+        keep = ctx.enter_context(tc.tile_pool(name="keep", bufs=1))
+        slots = ctx.enter_context(tc.tile_pool(name="slots", bufs=1))
+        ring = ctx.enter_context(tc.tile_pool(name="ring", bufs=3))
+        turn_banks = ctx.enter_context(tc.psum_pool(name="turn_banks", bufs=3))
+        sum_banks = ctx.enter_context(tc.psum_pool(name="sum_banks", bufs=1))
+
+        x_list = keep.tile([P, J // 16], U16, name="x_list")
+        z_list = keep.tile([P, J // 16], U16, name="z_list")
+        rows = [
+            slots.tile([P, K], F32, name="rows%d" % s, offset=s * SLOT, align_bytes=64) for s in range(2 * TILES)
+        ]
+        x_rows, z_rows = rows[0::2], rows[1::2]
+        wb_raw = keep.tile([P, PASSES * N], U16, name="wb_raw")
+        wb_raw_scale = keep.tile([P, PASSES * N], U8, name="wb_raw_scale")
+        wb_codes = keep.tile([P, PASSES * N], U16, name="wb_codes", align_bytes=64)
+        wb_scale = keep.tile([P, PASSES * N], U8, name="wb_scale", align_bytes=64)
+        xb_codes = keep.tile([P, PASSES * T], U16, name="xb_codes", align_bytes=64)
+        xb_scale = keep.tile([P, PASSES * T], U8, name="xb_scale", align_bytes=64)
+        vo_raw = keep.tile([P, N], U32, name="vo_raw")
+        vo_raw_scale = keep.tile([P, N], U8, name="vo_raw_scale")
+        vo_codes = keep.tile([P, N], U32, name="vo_codes", align_bytes=64)
+        vo_scale = keep.tile([P, N], U8, name="vo_scale", align_bytes=64)
+        wo_raw = keep.tile([P, PACK, N], F32, name="wo_raw")
+        wo_bf = keep.tile([P, N * PACK], BF16, name="wo_bf", align_bytes=64)
+        wo_codes = keep.tile([P, N], U32, name="wo_codes", align_bytes=64)
+        wo_scale = keep.tile([P, N], U8, name="wo_scale", align_bytes=64)
+        bias = keep.tile([P, PACK], F32, name="bias")
+        identity = keep.tile([P, P], F32, name="identity")
+        y_codes = keep.tile([P, T], U32, name="y_codes", align_bytes=64)
+        y_scale = keep.tile([P, T], U8, name="y_scale", align_bytes=64)
+
+        nc.vector.memset(wb_raw_scale[:].bitcast(I32), 0)
+        nc.gpsimd.memset(xb_scale[:].bitcast(I32), 0)
+        nc.vector.memset(vo_raw_scale[:].bitcast(I32), 0)
+        make_identity(nc, identity[:])
+
+        def load_words(tile, words):
+            nc.sync.dma_start(
+                out=tile[:].bitcast(I32).rearrange("p (z c) -> p z c", z=words.shape[0]),
+                in_=words.rearrange("z p c -> p z c").bitcast(I32),
+            )
+
+        def load_rows(tiles, stream, g):
+            nc.sync.dma_start(out=tiles[g][:], in_=stream[g * P : (g + 1) * P, :])
+
+        load_words(wb_raw, wb_words)
+        load_scale_rows(nc, wb_raw_scale, wb_scales)
+        load_words(xb_codes, xb_words)
+        nc.sync.dma_start(out=wo_raw[:], in_=wo.rearrange("(p t) n -> p t n", t=PACK))
+        load_words(vo_raw, vo_words.rearrange("z p c r -> z p (c r)"))
+        load_scale_rows(nc, xb_scale, xb_scales)
+        nc.sync.dma_start(out=x_list[:], in_=offs)
+        load_rows(x_rows, xt, 0)
+        nc.sync.dma_start(out=z_list[:], in_=offs2)
+        load_rows(z_rows, zt, 0)
+        load_scale_rows(nc, vo_raw_scale, vo_scales)
+        load_rows(x_rows, xt, 1)
+        nc.sync.dma_start(out=bias[:], in_=b.rearrange("(p i) one -> p (i one)", i=PACK))
+        load_rows(z_rows, zt, 1)
+        for g in range(2, TILES):
+            load_rows(x_rows, xt, g)
+            load_rows(z_rows, zt, g)
+
+        deal(nc.scalar.copy, wb_codes[:], wb_raw[:])
+        nc.vector.tensor_copy(
+            out=wo_bf[:].rearrange("p (i m t) -> p m t i", i=PACK, t=PACK),
+            in_=wo_raw[:].rearrange("p t (m i) -> p m t i", i=PACK),
+        )
+        deal(nc.vector.tensor_copy, wb_scale[:], wb_raw_scale[:])
+        nc.vector.quantize_mx(out=wo_codes[:].bitcast(FP8X4), scales=wo_scale[:], in_=wo_bf[:])
+        deal(nc.scalar.copy, vo_codes[:], vo_raw[:])
+        deal(nc.vector.tensor_copy, vo_scale[:], vo_raw_scale[:])
+
+        def add_pass(banks, lhsT, lhsT_scale, first, rhs, rhs_scale, dtype, start=False, stop=False):
+            per_bank = PACK // len(banks)
+            for i in range(PACK):
+                cols = slice(first + i * P, first + (i + 1) * P)
+                nc.tensor.matmul_mx(
+                    out=banks[i // per_bank][:, i % per_bank, :],
+                    lhsT=lhsT[:, cols].bitcast(dtype),
+                    lhsT_scale=lhsT_scale[:, cols],
+                    rhs=rhs.bitcast(dtype),
+                    rhs_scale=rhs_scale,
+                    start=start and i % per_bank == 0,
+                    stop=stop and i % per_bank == per_bank - 1,
+                )
+
+        def base_part(g):
+            count = 2 if g == LAST else 1
+            banks = [sum_banks.tile([P, PACK // count, P], F32, name="sums%d_%d" % (g, h)) for h in range(count)]
+            for z in range(PASSES):
+                tokens = slice(z * T + g * P, z * T + (g + 1) * P)
+                add_pass(banks, wb_codes, wb_scale, z * N, xb_codes[:, tokens], xb_scale[:, tokens], FP4X4, start=z == 0)
+            return banks
+
+        def pick_and_turn(s):
+            offsets = (x_list, z_list)[s % 2]
+            picked = ring.tile([P, J], BF16, name="picked", bufs=2)
+            half = J // 2
+            nc.vector.tensor_copy(out=picked[:, :half], in_=rows[s][:].indirect(offsets[:, : half // 16]))
+            nc.scalar.activation(out=picked[:, half:], in_=rows[s][:].indirect(offsets[:, half // 16 :]), func=ACT.Copy)
+            pairs = picked[:].bitcast(F32)
+            turned = turn_banks.tile([P, 2, P], F32, name="turned")
+            for u in range(2):
+                nc.tensor.transpose(turned[:, u, :], pairs[:, u : J // 2 : 2], identity[:])
+            return turned
+
+        def group(s, turned):
+            grouped = slots.tile([P, P * PACK], BF16, name="grouped%d" % s, offset=(s + 1) * SLOT, align_bytes=64)
+            nc.scalar.copy(
+                out=grouped[:].bitcast(F32).rearrange("p (c u) -> p c u", u=2),
+                in_=turned[:].rearrange("p u c -> p c u"),
+            )
+            return grouped
+
+        def multiply(s, grouped, banks):
+            codes = ring.tile([P, P], U32, name="codes", align_bytes=64)
+            scale = ring.tile([P, P], U8, name="scale", align_bytes=64)
+            nc.vector.quantize_mx(out=codes[:].bitcast(FP8X4), scales=scale[:], in_=grouped[:])
+            weight_codes, weight_scale = ((wo_codes, wo_scale), (vo_codes, vo_scale))[s % 2]
+            add_pass(banks, weight_codes, weight_scale, 0, codes[:], scale[:], FP8X4, stop=s % 2 == 1)
+
+        out_rows = out_0.rearrange("(p i) t -> p i t", i=PACK)
+        out_words = out_1[0].rearrange("p c r -> p (c r)").bitcast(I32)
+
+        def add_bias(g, banks):
+            y = slots.tile([P, PACK, P], F32, name="y%d" % g, offset=(2 * g + 3) * SLOT + SLOT // 2, align_bytes=64)
+            first = PACK - banks[-1].shape[1]
+            for i in range(first):
+                nc.scalar.activation(out=y[:, i, :], in_=banks[0][:, i, :], func=ACT.Identity, bias=bias[:, i : i + 1])
+            nc.vector.tensor_tensor(
+                out=y[:, first:, :],
+                in0=banks[-1][:],
+                in1=bias[:, first:].unsqueeze(2).to_broadcast([P, PACK - first, P]),
+                op=ADD,
+            )
+            nc.sync.dma_start(out=out_rows[:, :, g * P : (g + 1) * P], in_=y[:])
+            return y
+
+        def make_planes(g, y):
+            place = (2 * g + 4) * SLOT + (SLOT // 2 if g < LAST - 1 else 0)
+            y_bf = slots.tile([P, P * PACK], BF16, name="y_bf%d" % g, offset=place, align_bytes=64)
+            nc.vector.tensor_copy(out=y_bf[:].rearrange("p (c i) -> p c i", i=PACK), in_=y[:].rearrange("p i c -> p c i"))
+            tokens = slice(g * P, (g + 1) * P)
+            nc.vector.quantize_mx(out=y_codes[:, tokens].bitcast(FP8X4), scales=y_scale[:, tokens], in_=y_bf[:])
+
+        sums = [base_part(g) for g in range(TILES)]
+        steps = 2 * TILES
+        turned = pick_and_turn(0)
+        y = None
+        for s in range(1, steps):
+            turned_before, turned = turned, pick_and_turn(s)
+            if s >= 3 and s % 2 == 1:
+                y = add_bias(s // 2 - 1, sums[s // 2 - 1])
+            if s >= 4 and s % 2 == 0:
+                make_planes(s // 2 - 2, y)
+            multiply(s - 1, group(s - 1, turned_before), sums[(s - 1) // 2])
+        multiply(steps - 1, group(steps - 1, turned), sums[LAST])
+        make_planes(LAST - 1, y)
+        nc.sync.dma_start(out=out_words[:, : LAST * P], in_=y_codes[:, : LAST * P].bitcast(I32))
+        make_planes(LAST, add_bias(LAST, sums[LAST]))
+        nc.sync.dma_start(out=out_words[:, LAST * P :], in_=y_codes[:, LAST * P :].bitcast(I32))
+        for q in range(4):
+            queue = nc.sync if q < 2 else nc.scalar
+            queue.dma_start(
+                out=out_2[0, PACK * q : PACK * (q + 1), :].bitcast(I32),
+                in_=y_scale[32 * q : 32 * q + PACK, :].bitcast(I32),
+            )

@@ -50,8 +50,8 @@ def tile_list_outlier_streams_pl_kernel(
         keep = ctx.enter_context(tc.tile_pool(name="keep", bufs=1))
         slots = ctx.enter_context(tc.tile_pool(name="slots", bufs=1))
         ring = ctx.enter_context(tc.tile_pool(name="ring", bufs=3))
-        turn_banks = ctx.enter_context(tc.psum_pool(name="turn_banks", bufs=3))
-        sum_banks = ctx.enter_context(tc.psum_pool(name="sum_banks", bufs=1))
+        turn_banks = ctx.enter_context(tc.psum_pool(name="turn_banks", bufs=4))
+        sum_banks = ctx.enter_context(tc.psum_pool(name="sum_banks", bufs=2))
 
         x_list = keep.tile([P, J // 16], U16, name="x_list")
         z_list = keep.tile([P, J // 16], U16, name="z_list")
@@ -121,22 +121,20 @@ def tile_list_outlier_streams_pl_kernel(
         deal(nc.vector.tensor_copy, vo_scale[:], vo_raw_scale[:])
 
         def add_pass(banks, lhsT, lhsT_scale, first, rhs, rhs_scale, dtype, start=False, stop=False):
-            per_bank = PACK // len(banks)
             for i in range(PACK):
                 cols = slice(first + i * P, first + (i + 1) * P)
                 nc.tensor.matmul_mx(
-                    out=banks[i // per_bank][:, i % per_bank, :],
+                    out=banks[i // 2][:, i % 2, :],
                     lhsT=lhsT[:, cols].bitcast(dtype),
                     lhsT_scale=lhsT_scale[:, cols],
                     rhs=rhs.bitcast(dtype),
                     rhs_scale=rhs_scale,
-                    start=start and i % per_bank == 0,
-                    stop=stop and i % per_bank == per_bank - 1,
+                    start=start and i % 2 == 0,
+                    stop=stop and i % 2 == 1,
                 )
 
         def base_part(g):
-            count = 2 if g == LAST else 1
-            banks = [sum_banks.tile([P, PACK // count, P], F32, name="sums%d_%d" % (g, h)) for h in range(count)]
+            banks = [sum_banks.tile([P, 2, P], F32, name="sums%d" % h) for h in range(2)]
             for z in range(PASSES):
                 tokens = slice(z * T + g * P, z * T + (g + 1) * P)
                 add_pass(banks, wb_codes, wb_scale, z * N, xb_codes[:, tokens], xb_scale[:, tokens], FP4X4, start=z == 0)
@@ -174,40 +172,44 @@ def tile_list_outlier_streams_pl_kernel(
 
         def add_bias(g, banks):
             y = slots.tile([P, PACK, P], F32, name="y%d" % g, offset=(2 * g + 3) * SLOT + SLOT // 2, align_bytes=64)
-            first = PACK - banks[-1].shape[1]
-            for i in range(first):
+            for i in range(2):
                 nc.scalar.activation(out=y[:, i, :], in_=banks[0][:, i, :], func=ACT.Identity, bias=bias[:, i : i + 1])
             nc.vector.tensor_tensor(
-                out=y[:, first:, :],
-                in0=banks[-1][:],
-                in1=bias[:, first:].unsqueeze(2).to_broadcast([P, PACK - first, P]),
-                op=ADD,
+                out=y[:, 2:, :], in0=banks[1][:], in1=bias[:, 2:].unsqueeze(2).to_broadcast([P, 2, P]), op=ADD
             )
             nc.sync.dma_start(out=out_rows[:, :, g * P : (g + 1) * P], in_=y[:])
             return y
 
-        def make_planes(g, y):
+        def round_y(g, y):
             place = (2 * g + 4) * SLOT + (SLOT // 2 if g < LAST - 1 else 0)
             y_bf = slots.tile([P, P * PACK], BF16, name="y_bf%d" % g, offset=place, align_bytes=64)
             nc.vector.tensor_copy(out=y_bf[:].rearrange("p (c i) -> p c i", i=PACK), in_=y[:].rearrange("p i c -> p c i"))
+            return y_bf
+
+        def make_planes(g, y_bf):
             tokens = slice(g * P, (g + 1) * P)
             nc.vector.quantize_mx(out=y_codes[:, tokens].bitcast(FP8X4), scales=y_scale[:, tokens], in_=y_bf[:])
 
-        sums = [base_part(g) for g in range(TILES)]
         steps = 2 * TILES
+        sums = [base_part(0), base_part(1)]
         turned = pick_and_turn(0)
         y = None
         for s in range(1, steps):
             turned_before, turned = turned, pick_and_turn(s)
+            grouped = group(s - 1, turned_before)
             if s >= 3 and s % 2 == 1:
                 y = add_bias(s // 2 - 1, sums[s // 2 - 1])
             if s >= 4 and s % 2 == 0:
-                make_planes(s // 2 - 2, y)
-            multiply(s - 1, group(s - 1, turned_before), sums[(s - 1) // 2])
+                y_bf = round_y(s // 2 - 2, y)
+            multiply(s - 1, grouped, sums[(s - 1) // 2])
+            if s >= 4 and s % 2 == 0:
+                make_planes(s // 2 - 2, y_bf)
+            if s >= 3 and s % 2 == 1 and s // 2 + 1 < TILES:
+                sums.append(base_part(s // 2 + 1))
         multiply(steps - 1, group(steps - 1, turned), sums[LAST])
-        make_planes(LAST - 1, y)
+        make_planes(LAST - 1, round_y(LAST - 1, y))
         nc.sync.dma_start(out=out_words[:, : LAST * P], in_=y_codes[:, : LAST * P].bitcast(I32))
-        make_planes(LAST, add_bias(LAST, sums[LAST]))
+        make_planes(LAST, round_y(LAST, add_bias(LAST, sums[LAST])))
         nc.sync.dma_start(out=out_words[:, LAST * P :], in_=y_codes[:, LAST * P :].bitcast(I32))
         for q in range(4):
             queue = nc.sync if q < 2 else nc.scalar

@@ -29,7 +29,7 @@ def load_scale_rows(nc, plane, scales):
     passes = scales.shape[0]
     by_row = scales.rearrange("z (q r) c -> r q z c", r=PACK)
     for r in range(PACK):
-        nc.sync.dma_start(
+        nc.gpsimd.dma_start(
             out=plane[r:P:32, :].bitcast(I32).rearrange("q (z c) -> q z c", z=passes),
             in_=by_row[r].bitcast(I32),
         )
@@ -79,7 +79,7 @@ def tile_list_outlier_streams_pl_kernel(
         y_scale = keep.tile([P, T], U8, name="y_scale", align_bytes=64)
 
         nc.vector.memset(wb_raw_scale[:].bitcast(I32), 0)
-        nc.gpsimd.memset(xb_scale[:].bitcast(I32), 0)
+        nc.vector.memset(xb_scale[:].bitcast(I32), 0)
         nc.vector.memset(vo_raw_scale[:].bitcast(I32), 0)
         make_identity(nc, identity[:])
 
@@ -92,21 +92,17 @@ def tile_list_outlier_streams_pl_kernel(
         def load_rows(tiles, stream, g):
             nc.sync.dma_start(out=tiles[g][:], in_=stream[g * P : (g + 1) * P, :])
 
-        load_words(wb_raw, wb_words)
         load_scale_rows(nc, wb_raw_scale, wb_scales)
+        load_scale_rows(nc, xb_scale, xb_scales)
+        load_scale_rows(nc, vo_raw_scale, vo_scales)
+        load_words(wb_raw, wb_words)
         load_words(xb_codes, xb_words)
         nc.sync.dma_start(out=wo_raw[:], in_=wo.rearrange("(p t) n -> p t n", t=PACK))
         load_words(vo_raw, vo_words.rearrange("z p c r -> z p (c r)"))
-        load_scale_rows(nc, xb_scale, xb_scales)
         nc.sync.dma_start(out=x_list[:], in_=offs)
-        load_rows(x_rows, xt, 0)
         nc.sync.dma_start(out=z_list[:], in_=offs2)
-        load_rows(z_rows, zt, 0)
-        load_scale_rows(nc, vo_raw_scale, vo_scales)
-        load_rows(x_rows, xt, 1)
         nc.sync.dma_start(out=bias[:], in_=b.rearrange("(p i) one -> p (i one)", i=PACK))
-        load_rows(z_rows, zt, 1)
-        for g in range(2, TILES):
+        for g in range(TILES):
             load_rows(x_rows, xt, g)
             load_rows(z_rows, zt, g)
 

from contextlib import ExitStack

import concourse.mybir as mybir
from concourse.masks import make_identity

K, J, T, N = 2048, 512, 512, 512
FLOPS = 2 * (K + J + J) * T * N

F32 = mybir.dt.float32
BF16 = mybir.dt.bfloat16
I32 = mybir.dt.int32
U32 = mybir.dt.uint32
U16 = mybir.dt.uint16
U8 = mybir.dt.uint8
FP8X4 = mybir.dt.float8_e4m3fn_x4
FP4X4 = mybir.dt.float4_e2m1fn_x4
ACT = mybir.ActivationFunctionType
ADD = mybir.AluOpType.add

P = 128
PACK = 4
PASSES = K // (P * PACK)
TILES = T // P
LAST = TILES - 1
SLOT = 4 * K


def load_scale_rows(nc, plane, scales):
    passes = scales.shape[0]
    by_row = scales.rearrange("z (q r) c -> r q z c", r=PACK)
    for r in range(PACK):
        nc.gpsimd.dma_start(
            out=plane[r:P:32, :].bitcast(I32).rearrange("q (z c) -> q z c", z=passes),
            in_=by_row[r].bitcast(I32),
        )


def deal(copy, dealt, raw):
    copy(
        out=dealt.rearrange("p (z i m) -> p z i m", i=PACK, m=P),
        in_=raw.rearrange("p (z m i) -> p z i m", i=PACK, m=P),
    )


def tile_list_outlier_streams_pl_kernel(
    tc, xb_words, xb_scales, wb_words, wb_scales, xt, wo, zt, vo_words, vo_scales, b, offs, offs2, out_0, out_1, out_2
):
    nc = tc.nc
    with ExitStack() as ctx:
        keep = ctx.enter_context(tc.tile_pool(name="keep", bufs=1))
        slots = ctx.enter_context(tc.tile_pool(name="slots", bufs=1))
        ring = ctx.enter_context(tc.tile_pool(name="ring", bufs=3))
        turn_banks = ctx.enter_context(tc.psum_pool(name="turn_banks", bufs=4))
        sum_banks = ctx.enter_context(tc.psum_pool(name="sum_banks", bufs=2))

        x_list = keep.tile([P, J // 16], U16, name="x_list")
        z_list = keep.tile([P, J // 16], U16, name="z_list")
        rows = [
            slots.tile([P, K], F32, name="rows%d" % s, offset=s * SLOT, align_bytes=64) for s in range(2 * TILES)
        ]
        x_rows, z_rows = rows[0::2], rows[1::2]
        wb_raw = keep.tile([P, PASSES * N], U16, name="wb_raw")
        wb_raw_scale = keep.tile([P, PASSES * N], U8, name="wb_raw_scale")
        wb_codes = keep.tile([P, PASSES * N], U16, name="wb_codes", align_bytes=64)
        wb_scale = keep.tile([P, PASSES * N], U8, name="wb_scale", align_bytes=64)
        xb_codes = keep.tile([P, PASSES * T], U16, name="xb_codes", align_bytes=64)
        xb_scale = keep.tile([P, PASSES * T], U8, name="xb_scale", align_bytes=64)
        vo_raw = keep.tile([P, N], U32, name="vo_raw")
        vo_raw_scale = keep.tile([P, N], U8, name="vo_raw_scale")
        vo_codes = keep.tile([P, N], U32, name="vo_codes", align_bytes=64)
        vo_scale = keep.tile([P, N], U8, name="vo_scale", align_bytes=64)
        wo_raw = keep.tile([P, PACK, N], F32, name="wo_raw")
        wo_bf = keep.tile([P, N * PACK], BF16, name="wo_bf", align_bytes=64)
        wo_codes = keep.tile([P, N], U32, name="wo_codes", align_bytes=64)
        wo_scale = keep.tile([P, N], U8, name="wo_scale", align_bytes=64)
        bias = keep.tile([P, PACK], F32, name="bias")
        identity = keep.tile([P, P], F32, name="identity")
        y_codes = keep.tile([P, T], U32, name="y_codes", align_bytes=64)
        y_scale = keep.tile([P, T], U8, name="y_scale", align_bytes=64)

        nc.vector.memset(wb_raw_scale[:].bitcast(I32), 0)
        nc.vector.memset(xb_scale[:].bitcast(I32), 0)
        nc.vector.memset(vo_raw_scale[:].bitcast(I32), 0)
        make_identity(nc, identity[:])

        def load_words(tile, words):
            nc.sync.dma_start(
                out=tile[:].bitcast(I32).rearrange("p (z c) -> p z c", z=words.shape[0]),
                in_=words.rearrange("z p c -> p z c").bitcast(I32),
            )

        def load_rows(tiles, stream, g):
            nc.sync.dma_start(out=tiles[g][:], in_=stream[g * P : (g + 1) * P, :])

        load_scale_rows(nc, wb_raw_scale, wb_scales)
        load_scale_rows(nc, xb_scale, xb_scales)
        load_scale_rows(nc, vo_raw_scale, vo_scales)
        load_words(wb_raw, wb_words)
        load_words(xb_codes, xb_words)
        nc.sync.dma_start(out=wo_raw[:], in_=wo.rearrange("(p t) n -> p t n", t=PACK))
        load_words(vo_raw, vo_words.rearrange("z p c r -> z p (c r)"))
        nc.sync.dma_start(out=x_list[:], in_=offs)
        nc.sync.dma_start(out=z_list[:], in_=offs2)
        nc.sync.dma_start(out=bias[:], in_=b.rearrange("(p i) one -> p (i one)", i=PACK))
        for g in range(TILES):
            load_rows(x_rows, xt, g)
            load_rows(z_rows, zt, g)

        deal(nc.scalar.copy, wb_codes[:], wb_raw[:])
        nc.vector.tensor_copy(
            out=wo_bf[:].rearrange("p (i m t) -> p m t i", i=PACK, t=PACK),
            in_=wo_raw[:].rearrange("p t (m i) -> p m t i", i=PACK),
        )
        deal(nc.vector.tensor_copy, wb_scale[:], wb_raw_scale[:])
        nc.vector.quantize_mx(out=wo_codes[:].bitcast(FP8X4), scales=wo_scale[:], in_=wo_bf[:])
        deal(nc.scalar.copy, vo_codes[:], vo_raw[:])
        deal(nc.vector.tensor_copy, vo_scale[:], vo_raw_scale[:])

        def add_pass(banks, lhsT, lhsT_scale, first, rhs, rhs_scale, dtype, start=False, stop=False):
            for i in range(PACK):
                cols = slice(first + i * P, first + (i + 1) * P)
                nc.tensor.matmul_mx(
                    out=banks[i // 2][:, i % 2, :],
                    lhsT=lhsT[:, cols].bitcast(dtype),
                    lhsT_scale=lhsT_scale[:, cols],
                    rhs=rhs.bitcast(dtype),
                    rhs_scale=rhs_scale,
                    start=start and i % 2 == 0,
                    stop=stop and i % 2 == 1,
                )

        def base_part(g):
            banks = [sum_banks.tile([P, 2, P], F32, name="sums%d" % h) for h in range(2)]
            for z in range(PASSES):
                tokens = slice(z * T + g * P, z * T + (g + 1) * P)
                add_pass(banks, wb_codes, wb_scale, z * N, xb_codes[:, tokens], xb_scale[:, tokens], FP4X4, start=z == 0)
            return banks

        def pick_and_turn(s):
            offsets = (x_list, z_list)[s % 2]
            picked = ring.tile([P, J], BF16, name="picked", bufs=2)
            half = J // 2
            nc.vector.tensor_copy(out=picked[:, :half], in_=rows[s][:].indirect(offsets[:, : half // 16]))
            nc.scalar.activation(out=picked[:, half:], in_=rows[s][:].indirect(offsets[:, half // 16 :]), func=ACT.Copy)
            pairs = picked[:].bitcast(F32)
            turned = turn_banks.tile([P, 2, P], F32, name="turned")
            for u in range(2):
                nc.tensor.transpose(turned[:, u, :], pairs[:, u : J // 2 : 2], identity[:])
            return turned

        def group(s, turned):
            grouped = slots.tile([P, P * PACK], BF16, name="grouped%d" % s, offset=(s + 1) * SLOT, align_bytes=64)
            nc.scalar.copy(
                out=grouped[:].bitcast(F32).rearrange("p (c u) -> p c u", u=2),
                in_=turned[:].rearrange("p u c -> p c u"),
            )
            return grouped

        def multiply(s, grouped, banks):
            codes = ring.tile([P, P], U32, name="codes", align_bytes=64)
            scale = ring.tile([P, P], U8, name="scale", align_bytes=64)
            nc.vector.quantize_mx(out=codes[:].bitcast(FP8X4), scales=scale[:], in_=grouped[:])
            weight_codes, weight_scale = ((wo_codes, wo_scale), (vo_codes, vo_scale))[s % 2]
            add_pass(banks, weight_codes, weight_scale, 0, codes[:], scale[:], FP8X4, stop=s % 2 == 1)

        out_rows = out_0.rearrange("(p i) t -> p i t", i=PACK)
        out_words = out_1[0].rearrange("p c r -> p (c r)").bitcast(I32)

        def add_bias(g, banks):
            y = slots.tile([P, PACK, P], F32, name="y%d" % g, offset=(2 * g + 3) * SLOT + SLOT // 2, align_bytes=64)
            for i in range(2):
                nc.scalar.activation(out=y[:, i, :], in_=banks[0][:, i, :], func=ACT.Identity, bias=bias[:, i : i + 1])
            nc.vector.tensor_tensor(
                out=y[:, 2:, :], in0=banks[1][:], in1=bias[:, 2:].unsqueeze(2).to_broadcast([P, 2, P]), op=ADD
            )
            nc.sync.dma_start(out=out_rows[:, :, g * P : (g + 1) * P], in_=y[:])
            return y

        def round_y(g, y):
            place = (2 * g + 4) * SLOT + (SLOT // 2 if g < LAST - 1 else 0)
            y_bf = slots.tile([P, P * PACK], BF16, name="y_bf%d" % g, offset=place, align_bytes=64)
            nc.vector.tensor_copy(out=y_bf[:].rearrange("p (c i) -> p c i", i=PACK), in_=y[:].rearrange("p i c -> p c i"))
            return y_bf

        def make_planes(g, y_bf):
            tokens = slice(g * P, (g + 1) * P)
            nc.vector.quantize_mx(out=y_codes[:, tokens].bitcast(FP8X4), scales=y_scale[:, tokens], in_=y_bf[:])

        steps = 2 * TILES
        sums = [base_part(0), base_part(1)]
        turned = pick_and_turn(0)
        y = None
        for s in range(1, steps):
            turned_before, turned = turned, pick_and_turn(s)
            grouped = group(s - 1, turned_before)
            if s >= 3 and s % 2 == 1:
                y = add_bias(s // 2 - 1, sums[s // 2 - 1])
            if s >= 4 and s % 2 == 0:
                y_bf = round_y(s // 2 - 2, y)
            multiply(s - 1, grouped, sums[(s - 1) // 2])
            if s >= 4 and s % 2 == 0:
                make_planes(s // 2 - 2, y_bf)
            if s >= 3 and s % 2 == 1 and s // 2 + 1 < TILES:
                sums.append(base_part(s // 2 + 1))
        multiply(steps - 1, group(steps - 1, turned), sums[LAST])
        make_planes(LAST - 1, round_y(LAST - 1, y))
        nc.sync.dma_start(out=out_words[:, : LAST * P], in_=y_codes[:, : LAST * P].bitcast(I32))
        make_planes(LAST, round_y(LAST, add_bias(LAST, sums[LAST])))
        nc.sync.dma_start(out=out_words[:, LAST * P :], in_=y_codes[:, LAST * P :].bitcast(I32))
        for q in range(4):
            queue = nc.sync if q < 2 else nc.scalar
            queue.dma_start(
                out=out_2[0, PACK * q : PACK * (q + 1), :].bitcast(I32),
                in_=y_scale[32 * q : 32 * q + PACK, :].bitcast(I32),
            )
